import numpy as np
import ml_dtypes


def mxq(x, axis, fmt="e4m3"):
    dtype, down = {"e4m3": (ml_dtypes.float8_e4m3fn, 7), "e5m2": (ml_dtypes.float8_e5m2, 14)}[fmt]
    v = np.moveaxis(np.asarray(x, np.float32).astype(ml_dtypes.bfloat16).astype(np.float64), axis, -1)
    blocks = v.reshape(v.shape[:-1] + (-1, 32))
    amax = np.abs(blocks).max(-1, keepdims=True)
    byte = np.maximum(np.where(amax > 0, np.frexp(amax)[1] - 1 + 127, 0) - down, 1)
    scale = np.exp2(byte - 127.0)
    codes = (blocks / scale).astype(np.float32).astype(dtype).astype(np.float64)
    return np.moveaxis((codes * scale).reshape(v.shape), -1, axis)


WIDE = False


def mx_kscale(k):
    if not WIDE:
        return np.ones(k)
    levels = np.array([10, -10, 5, -5, 0])
    if k % 512:
        return np.exp2(np.random.permutation(np.resize(levels, k // 32))).repeat(32)
    a = np.empty((k // 512, 16))
    for p in range(k // 512):
        a[p, :8] = np.random.permutation(np.resize(levels, 8))
        for g in range(8):
            far = levels[np.abs(levels - a[p, g]) >= 10]
            a[p, g + 8] = far[np.random.randint(len(far))]
    return np.exp2(a.ravel()).repeat(32)


def f64(x):
    return np.asarray(x).astype(np.float64)


def striped(idx):
    return np.tile(idx.reshape(-1, 16).T, (8, 1)).astype(np.uint16)


def unstriped(offs):
    return offs[:16].T.reshape(-1).astype(np.int64)


def striped8(idx):
    return np.concatenate([x.reshape(-1, 16).T for x in idx]).astype(np.uint16)


def runs(offs, k):
    lists = np.stack([offs[16 * r : 16 * r + 16].T.reshape(-1) for r in range(8)]).astype(np.int64)
    return lists[np.arange(k) % 512 // 64]


def pack_weight(w):
    k, n = w.shape
    w = f64(np.asarray(w, np.float32).astype(ml_dtypes.bfloat16)).reshape(k // 32, 32, n)
    amax = np.abs(w).max(1)
    byte = np.clip(np.where(amax > 0, np.frexp(amax)[1] - 1 + 127 - 7, 1), 1, 254)
    scaled = (w * np.exp2(127.0 - byte)[:, None, :]).reshape(k, n).astype(np.float32)
    words = np.ascontiguousarray(scaled.reshape(k // 512, 128, 4, n).transpose(0, 1, 3, 2)).astype(ml_dtypes.float8_e4m3fn).view(np.uint8)
    return words, np.ascontiguousarray(byte.astype(np.uint8).reshape(k // 512, 16, n))


def unpack_weight(words, scales):
    g, p, n, _ = words.shape
    vals = np.ascontiguousarray(words).view(ml_dtypes.float8_e4m3fn).astype(np.float64) * np.repeat(np.exp2(scales.astype(np.float64) - 127.0), 8, axis=1)[..., None]
    return vals.transpose(0, 1, 3, 2).reshape(g * 512, n)


def sigmoid(v):
    return 1.0 / (1.0 + np.exp(-np.maximum(v, -700.0)))


K, T, S, N, H = 512, 2048, 512, 512, 512


def setup_inputs():
    n = np.random.standard_normal
    s = mx_kscale(K)[:, None]
    u = mx_kscale(S)
    packed_xT = pack_weight(n((K, T)) * s)
    return {
        "x_words": packed_xT[0],
        "x_scales": packed_xT[1],
        "wa": (n((K, H)) / np.sqrt(K) / s).astype(np.float32),
        "wb": (n((K, N)) / np.sqrt(K) / s).astype(np.float32),
        "gt": (np.random.uniform(0.5, 1.5, (S, 1)) * u[:, None]).astype(np.float32),
        "gi": (np.random.uniform(0.5, 1.5, (S, 1)) / u[:, None]).astype(np.float32),
        "offs": striped(np.random.permutation(T)[:S]),
        "two": striped(np.random.permutation(T)[:S]),
        "n1": striped8(np.stack([np.random.permutation(H) for _ in range(8)])),
        "n2": striped8(np.stack([np.random.permutation(H) for _ in range(8)])),
        "n3": striped8(np.stack([np.random.permutation(N) for _ in range(8)])),
        "n4": striped8(np.stack([np.random.permutation(N) for _ in range(8)])),
    }


def reference(x_words, x_scales, wa, wb, gt, gi, offs, two, n1, n2, n3, n4):
    xq = unpack_weight(x_words, x_scales)[:, unstriped(offs)]
    a = xq.T @ mxq(f64(wa), 0, "e4m3")
    st = a[np.arange(S)[:, None], runs(n1, S)] - a
    z = f64(gt) * (a * (sigmoid(st[np.arange(S)[:, None], runs(n2, S)])))
    x_two = unpack_weight(x_words, x_scales)[:, unstriped(two)]
    b = x_two.T @ mxq(f64(wb), 0, "e4m3")
    z2 = f64(gi) * b
    cv = 0.0625 * ((mxq(z, 0, "e4m3").T @ mxq(z2, 0, "e4m3")))
    st2 = np.maximum(cv, cv[np.arange(H)[:, None], runs(n3, H)])
    return st2[np.arange(H)[:, None], runs(n4, H)] - (0.5 * cv)

@@ -1,0 +1,196 @@
+from contextlib import ExitStack
+
+import concourse.mybir as mybir
+from concourse.masks import make_identity
+
+K, T, S, N, H = 512, 2048, 512, 512, 512
+FLOPS = 2 * K * S * H + 2 * K * S * N + 2 * S * H * N
+
+F32 = mybir.dt.float32
+BF16 = mybir.dt.bfloat16
+I32 = mybir.dt.int32
+U32 = mybir.dt.uint32
+U16 = mybir.dt.uint16
+U8 = mybir.dt.uint8
+FP8X4 = mybir.dt.float8_e4m3fn_x4
+ALU = mybir.AluOpType
+ACT = mybir.ActivationFunctionType
+
+P = 128
+PACK = 4
+W = 512
+
+
+def tile_picked_momhopdhopb_none_p_kernel(
+    tc, x_words, x_scales, wa, wb, gt, gi, offs, two, n1, n2, n3, n4, out
+):
+    nc = tc.nc
+    with ExitStack() as ctx:
+        keep = ctx.enter_context(tc.tile_pool(name="keep", bufs=1))
+        psum = ctx.enter_context(tc.psum_pool(name="psum", bufs=1))
+
+        def sb(name, shape, dtype):
+            return keep.tile(shape, dtype, name=name, align_bytes=64)
+
+        lists = {}
+        for name in ("offs", "two", "n1", "n2", "n3", "n4"):
+            lists[name] = sb("list_" + name, [P, W // 16], U16)
+
+        xs = sb("xs", [P, T], U8)
+        xw = sb("xw", [P, T], I32)
+        wa_raw = sb("wa_raw", [P, PACK, H], F32)
+        wb_raw = sb("wb_raw", [P, PACK, N], F32)
+        gains_in = sb("gains_in", [P, P], F32)
+        gains = sb("gains", [P, 2 * PACK], F32)
+        ident = sb("ident", [P, P], F32)
+        first = [sb("first%d" % t, [P, 2 * W], F32) for t in range(PACK)]
+        second = [sb("second%d" % t, [P, 2 * W], F32) for t in range(PACK)]
+
+        nc.vector.memset(xs[:].bitcast(I32), 0)
+        warm = sb("warm", [P, 2], F32)
+        nc.gpsimd.memset(warm[:, 0:1], 0.0)
+        nc.scalar.activation(warm[:, 1:2], warm[:, 0:1], ACT.Sigmoid)
+        for t in range(PACK):
+            nc.vector.memset(first[t][:, W:], 0.0)
+        nc.gpsimd.memset(gains_in[:], 0.0)
+        make_identity(nc, ident[:])
+
+        nc.sync.dma_start(lists["offs"][:], offs)
+        nc.sync.dma_start(lists["two"][:], two)
+        for q in range(4):
+            nc.sync.dma_start(xs[32 * q : 32 * q + 4, :].bitcast(I32), x_scales[0, 4 * q : 4 * q + 4, :].bitcast(I32))
+        nc.sync.dma_start(wa_raw[:], wa.rearrange("(p j) c -> p j c", j=PACK))
+        nc.sync.dma_start(xw[:], x_words[0].rearrange("p n r -> p (n r)").bitcast(I32))
+        nc.sync.dma_start(wb_raw[:], wb.rearrange("(p j) c -> p j c", j=PACK))
+        nc.sync.dma_start(lists["n1"][:], n1)
+        nc.sync.dma_start(lists["n2"][:], n2)
+        for j, gain in enumerate((gt, gi)):
+            nc.sync.dma_start(
+                gains_in[PACK * j : PACK * (j + 1), :].rearrange("t (h e) -> t h e", e=8),
+                gain.rearrange("(h t e) o -> t h (e o)", t=PACK, e=8),
+            )
+        nc.sync.dma_start(lists["n3"][:], n3)
+        nc.sync.dma_start(lists["n4"][:], n4)
+
+        def pick_scales(name):
+            got = sb("got_" + name, [P, S], U8)
+            nc.vector.tensor_copy(got[:], xs[:].indirect(lists[name][:]))
+            dealt = sb("xs_" + name, [P, S], U8)
+            nc.vector.tensor_copy(
+                dealt[:].bitcast(I32).rearrange("p (t h e) -> p t h e", t=PACK, e=2),
+                got[:].bitcast(I32).rearrange("p (h t e) -> p t h e", t=PACK, e=2),
+            )
+            return dealt
+
+        def pick_words(name):
+            dealt = sb("xw_" + name, [P, S], U32)
+            nc.vector.tensor_copy(
+                dealt[:].rearrange("p (t h e) -> p h t e", t=PACK, e=8),
+                xw[:].bitcast(U32).indirect(lists[name][:]),
+            )
+            return dealt
+
+        def weave(copy, name, raw, c0, c1):
+            woven = sb(name, [P, (c1 - c0) * PACK], BF16)
+            copy(
+                woven[:].rearrange("p (c i j) -> p c j i", i=4, j=PACK),
+                raw[:, :, c0:c1].rearrange("p j (c i) -> p c j i", i=4),
+            )
+            return woven
+
+        def quantise(codes, scales, woven):
+            nc.vector.quantize_mx(out=codes.bitcast(FP8X4), scales=scales, in_=woven)
+
+        def product(bank, lw, ls, rw, rs):
+            nc.tensor.matmul_mx(out=bank, lhsT=lw.bitcast(FP8X4), lhsT_scale=ls, rhs=rw.bitcast(FP8X4), rhs_scale=rs, start=True, stop=True)
+
+        def quantise_weight(name, raw):
+            codes = sb(name + "_codes", [P, W], U32)
+            scales = sb(name + "_scales", [P, W], U8)
+            half = W // 2
+            lo = weave(nc.scalar.copy, name + "_lo", raw, 0, half)
+            hi = weave(nc.vector.tensor_copy, name + "_hi", raw, half, W)
+            quantise(codes[:, half:], scales[:, half:], hi[:])
+            quantise(codes[:, :half], scales[:, :half], lo[:])
+            return codes, scales
+
+        xs_a = pick_scales("offs")
+        xs_b = pick_scales("two")
+        wa_codes, wa_scales = quantise_weight("wa", wa_raw)
+        xw_a = pick_words("offs")
+
+        banks_a = [psum.tile([P, W], F32, name="bank_a%d" % t) for t in range(PACK)]
+        banks_b = [psum.tile([P, PACK, P], F32, name="bank_b%d" % c) for c in range(PACK)]
+        for t in range(PACK):
+            cols = slice(t * P, (t + 1) * P)
+            product(banks_a[t][:], xw_a[:, cols], xs_a[:, cols], wa_codes[:], wa_scales[:])
+        xw_b = pick_words("two")
+        nc.tensor.transpose(banks_b[0][:, 0, :], gains_in[:], ident[:])
+        nc.scalar.copy(gains[:], banks_b[0][:, 0, : 2 * PACK])
+
+        sig = sb("sig", [P, PACK, W], F32)
+        ga = sb("ga", [P, PACK, W], F32)
+        for t in range(PACK):
+            nc.scalar.copy(first[t][:, :W], banks_a[t][:])
+            nc.scalar.copy(second[t][:, W:], banks_a[t][:])
+            nc.vector.tensor_tensor(second[t][:, :W], first[t][:].indirect(lists["n1"][:]), second[t][:, W:], ALU.subtract)
+        wb_codes, wb_scales = quantise_weight("wb", wb_raw)
+        for t in range(PACK):
+            nc.scalar.activation(sig[:, t, :], second[t][:].indirect(lists["n2"][:]), ACT.Sigmoid)
+            nc.scalar.activation(ga[:, t, :], banks_a[t][:], ACT.Copy, scale=gains[:, t : t + 1])
+
+        z2 = sb("z2", [P, N, PACK], BF16)
+        for c in range(PACK):
+            ccols = slice(c * P, (c + 1) * P)
+            for t in range(PACK):
+                cols = slice(t * P, (t + 1) * P)
+                product(banks_b[c][:, t, :], xw_b[:, cols], xs_b[:, cols], wb_codes[:, ccols], wb_scales[:, ccols])
+            nc.vector.tensor_tensor(
+                z2[:, ccols, :],
+                banks_b[c][:].rearrange("p t n -> p n t"),
+                gains[:, PACK:].unsqueeze(1).to_broadcast([P, P, PACK]),
+                ALU.mult,
+            )
+        z2_codes = sb("z2_codes", [P, N], U32)
+        z2_scales = sb("z2_scales", [P, N], U8)
+        quantise(z2_codes[:], z2_scales[:], z2[:].rearrange("p n t -> p (n t)"))
+
+        z_tiles = []
+        for u in range(PACK):
+            z = sb("z%d" % u, [P, P * PACK], BF16)
+            nc.vector.tensor_tensor(
+                z[:].rearrange("p (g i t) -> p g t i", i=4, t=PACK),
+                sig[:].rearrange("p t (g u i) -> p u g t i", u=PACK, i=4)[:, u],
+                ga[:].rearrange("p t (g u i) -> p u g t i", u=PACK, i=4)[:, u],
+                ALU.mult,
+            )
+            z_tiles.append(z)
+        for u in range(PACK):
+            z_codes = sb("z_codes%d" % u, [P, P], U32)
+            z_scales = sb("z_scales%d" % u, [P, P], U8)
+            quantise(z_codes[:], z_scales[:], z_tiles[u][:])
+            product(banks_a[u][:], z_codes[:], z_scales[:], z2_codes[:], z2_scales[:])
+
+        rows = out.rearrange("(g u i) n -> u g i n", u=PACK, i=4)
+        fetched = [sb("fetched%d" % u, [P, W], F32) for u in range(PACK)]
+        result = [sb("result%d" % u, [P, W], F32) for u in range(PACK)]
+
+        def fetch(u):
+            nc.scalar.activation(first[u][:, :W], banks_a[u][:], ACT.Copy, scale=0.0625)
+            nc.vector.tensor_copy(fetched[u][:], first[u][:].indirect(lists["n3"][:]))
+            nc.scalar.activation(first[u][:, W:], banks_a[u][:], ACT.Copy, scale=0.03125)
+
+        def larger(u):
+            nc.vector.tensor_tensor(second[u][:, :W], fetched[u][:], first[u][:, :W], ALU.max)
+
+        def finish(u):
+            nc.vector.tensor_tensor(result[u][:], second[u][:].indirect(lists["n4"][:]), first[u][:, W:], ALU.subtract)
+            nc.sync.dma_start(rows[u], result[u][:])
+
+        for step in range(PACK + 2):
+            if step < PACK:
+                fetch(step)
+            if 1 <= step <= PACK:
+                larger(step - 1)
+            if step >= 2:
+                finish(step - 2)

@@ -19,6 +19,7 @@ ACT = mybir.ActivationFunctionType
 P = 128
 PACK = 4
 W = 512
+HALF = W // 2
 
 
 def tile_picked_momhopdhopb_none_p_kernel(
@@ -29,8 +30,8 @@ def tile_picked_momhopdhopb_none_p_kernel(
         keep = ctx.enter_context(tc.tile_pool(name="keep", bufs=1))
         psum = ctx.enter_context(tc.psum_pool(name="psum", bufs=1))
 
-        def sb(name, shape, dtype):
-            return keep.tile(shape, dtype, name=name, align_bytes=64)
+        def sb(name, shape, dtype, tag=None):
+            return keep.tile(shape, dtype, name=name, tag=tag or name, align_bytes=64)
 
         lists = {}
         for name in ("offs", "two", "n1", "n2", "n3", "n4"):
@@ -38,8 +39,8 @@ def tile_picked_momhopdhopb_none_p_kernel(
 
         xs = sb("xs", [P, T], U8)
         xw = sb("xw", [P, T], I32)
-        wa_raw = sb("wa_raw", [P, PACK, H], F32)
-        wb_raw = sb("wb_raw", [P, PACK, N], F32)
+        wa_raw = [sb("wa_raw%d" % h, [P, PACK, HALF], F32) for h in range(2)]
+        wb_raw = [sb("wb_raw%d" % h, [P, PACK, HALF], F32) for h in range(2)]
         gains_in = sb("gains_in", [P, P], F32)
         gains = sb("gains", [P, 2 * PACK], F32)
         ident = sb("ident", [P, P], F32)
@@ -54,26 +55,32 @@ def tile_picked_momhopdhopb_none_p_kernel(
             nc.vector.memset(first[t][:, W:], 0.0)
         nc.gpsimd.memset(gains_in[:], 0.0)
         make_identity(nc, ident[:])
+        nc.gpsimd.memset(second[PACK - 1][:, W:], 0.0)
 
-        nc.sync.dma_start(lists["offs"][:], offs)
-        nc.sync.dma_start(lists["two"][:], two)
+        def load_half(tile, w, h):
+            nc.sync.dma_start(tile[:], w.rearrange("(p j) c -> p j c", j=PACK)[:, :, h * HALF : (h + 1) * HALF])
+
+        load_half(wa_raw[0], wa, 0)
         for q in range(4):
             nc.sync.dma_start(xs[32 * q : 32 * q + 4, :].bitcast(I32), x_scales[0, 4 * q : 4 * q + 4, :].bitcast(I32))
-        nc.sync.dma_start(wa_raw[:], wa.rearrange("(p j) c -> p j c", j=PACK))
+        nc.sync.dma_start(lists["offs"][:], offs)
+        load_half(wa_raw[1], wa, 1)
         nc.sync.dma_start(xw[:], x_words[0].rearrange("p n r -> p (n r)").bitcast(I32))
-        nc.sync.dma_start(wb_raw[:], wb.rearrange("(p j) c -> p j c", j=PACK))
-        nc.sync.dma_start(lists["n1"][:], n1)
-        nc.sync.dma_start(lists["n2"][:], n2)
+        nc.sync.dma_start(lists["two"][:], two)
         for j, gain in enumerate((gt, gi)):
             nc.sync.dma_start(
                 gains_in[PACK * j : PACK * (j + 1), :].rearrange("t (h e) -> t h e", e=8),
                 gain.rearrange("(h t e) o -> t h (e o)", t=PACK, e=8),
             )
+        load_half(wb_raw[0], wb, 0)
+        load_half(wb_raw[1], wb, 1)
+        nc.sync.dma_start(lists["n1"][:], n1)
+        nc.sync.dma_start(lists["n2"][:], n2)
         nc.sync.dma_start(lists["n3"][:], n3)
         nc.sync.dma_start(lists["n4"][:], n4)
 
-        def pick_scales(name):
-            got = sb("got_" + name, [P, S], U8)
+        def pick_scales(name, tag=None):
+            got = sb("got_" + name, [P, S], U8, tag)
             nc.vector.tensor_copy(got[:], xs[:].indirect(lists[name][:]))
             dealt = sb("xs_" + name, [P, S], U8)
             nc.vector.tensor_copy(
@@ -82,19 +89,19 @@ def tile_picked_momhopdhopb_none_p_kernel(
             )
             return dealt
 
-        def pick_words(name):
-            dealt = sb("xw_" + name, [P, S], U32)
+        def pick_words(name, tag=None):
+            dealt = sb("xw_" + name, [P, S], U32, tag)
             nc.vector.tensor_copy(
                 dealt[:].rearrange("p (t h e) -> p h t e", t=PACK, e=8),
                 xw[:].bitcast(U32).indirect(lists[name][:]),
             )
             return dealt
 
-        def weave(copy, name, raw, c0, c1):
-            woven = sb(name, [P, (c1 - c0) * PACK], BF16)
+        def weave(copy, name, raw):
+            woven = sb(name, [P, HALF * PACK], BF16)
             copy(
                 woven[:].rearrange("p (c i j) -> p c j i", i=4, j=PACK),
-                raw[:, :, c0:c1].rearrange("p j (c i) -> p c j i", i=4),
+                raw[:].rearrange("p j (c i) -> p c j i", i=4),
             )
             return woven
 
@@ -104,42 +111,51 @@ def tile_picked_momhopdhopb_none_p_kernel(
         def product(bank, lw, ls, rw, rs):
             nc.tensor.matmul_mx(out=bank, lhsT=lw.bitcast(FP8X4), lhsT_scale=ls, rhs=rw.bitcast(FP8X4), rhs_scale=rs, start=True, stop=True)
 
-        def quantise_weight(name, raw):
-            codes = sb(name + "_codes", [P, W], U32)
-            scales = sb(name + "_scales", [P, W], U8)
-            half = W // 2
-            lo = weave(nc.scalar.copy, name + "_lo", raw, 0, half)
-            hi = weave(nc.vector.tensor_copy, name + "_hi", raw, half, W)
-            quantise(codes[:, half:], scales[:, half:], hi[:])
-            quantise(codes[:, :half], scales[:, :half], lo[:])
-            return codes, scales
-
         xs_a = pick_scales("offs")
         xs_b = pick_scales("two")
-        wa_codes, wa_scales = quantise_weight("wa", wa_raw)
+        wa_codes = sb("wa_codes", [P, W], U32)
+        wa_scales = sb("wa_scales", [P, W], U8)
+        wa_lo = weave(nc.scalar.copy, "wa_lo", wa_raw[0])
+        wa_hi = weave(nc.scalar.copy, "wa_hi", wa_raw[1])
+        quantise(wa_codes[:, :HALF], wa_scales[:, :HALF], wa_lo[:])
+        quantise(wa_codes[:, HALF:], wa_scales[:, HALF:], wa_hi[:])
         xw_a = pick_words("offs")
+        xw_b = pick_words("two")
 
         banks_a = [psum.tile([P, W], F32, name="bank_a%d" % t) for t in range(PACK)]
         banks_b = [psum.tile([P, PACK, P], F32, name="bank_b%d" % c) for c in range(PACK)]
-        for t in range(PACK):
+        for t in (1, 2, 3, 0):
             cols = slice(t * P, (t + 1) * P)
             product(banks_a[t][:], xw_a[:, cols], xs_a[:, cols], wa_codes[:], wa_scales[:])
-        xw_b = pick_words("two")
-        nc.tensor.transpose(banks_b[0][:, 0, :], gains_in[:], ident[:])
-        nc.scalar.copy(gains[:], banks_b[0][:, 0, : 2 * PACK])
+        nc.tensor.transpose(banks_b[3][:, 0, :], gains_in[:], ident[:])
 
         sig = sb("sig", [P, PACK, W], F32)
         ga = sb("ga", [P, PACK, W], F32)
-        for t in range(PACK):
+        fetched = [sb("fetched%d" % u, [P, W], F32) for u in range(PACK)]
+        last_a = sb("last_a", [P, W], F32)
+        again = [second[t][:, W:] for t in range(PACK - 1)] + [last_a[:]]
+        for t in (1, 2, 3, 0):
             nc.scalar.copy(first[t][:, :W], banks_a[t][:])
-            nc.scalar.copy(second[t][:, W:], banks_a[t][:])
-            nc.vector.tensor_tensor(second[t][:, :W], first[t][:].indirect(lists["n1"][:]), second[t][:, W:], ALU.subtract)
-        wb_codes, wb_scales = quantise_weight("wb", wb_raw)
+            if t > 0:
+                nc.sync.dma_start(again[t], first[t][:, :W])
+            else:
+                nc.scalar.copy(again[t], banks_a[t][:])
+        for t in range(PACK):
+            nc.vector.tensor_tensor(second[t][:, :W], first[t][:].indirect(lists["n1"][:]), again[t], ALU.subtract)
+        nc.scalar.copy(gains[:], banks_b[3][:, 0, : 2 * PACK])
+        for t in range(PACK):
+            nc.scalar.activation(ga[:, t, :], banks_a[t][:], ACT.Copy, scale=gains[:, t : t + 1])
         for t in range(PACK):
             nc.scalar.activation(sig[:, t, :], second[t][:].indirect(lists["n2"][:]), ACT.Sigmoid)
-            nc.scalar.activation(ga[:, t, :], banks_a[t][:], ACT.Copy, scale=gains[:, t : t + 1])
 
-        z2 = sb("z2", [P, N, PACK], BF16)
+        wb_codes = sb("wb_codes", [P, W], U32)
+        wb_scales = sb("wb_scales", [P, W], U8)
+        wb_lo = weave(nc.vector.tensor_copy, "wb_lo", wb_raw[0])
+        wb_hi = weave(nc.vector.tensor_copy, "wb_hi", wb_raw[1])
+        quantise(wb_codes[:, :HALF], wb_scales[:, :HALF], wb_lo[:])
+        quantise(wb_codes[:, HALF:], wb_scales[:, HALF:], wb_hi[:])
+
+        z2 = sb("z2", [P, N, PACK], BF16, "last_a")
         for c in range(PACK):
             ccols = slice(c * P, (c + 1) * P)
             for t in range(PACK):
@@ -155,24 +171,29 @@ def tile_picked_momhopdhopb_none_p_kernel(
         z2_scales = sb("z2_scales", [P, N], U8)
         quantise(z2_codes[:], z2_scales[:], z2[:].rearrange("p n t -> p (n t)"))
 
-        z_tiles = []
-        for u in range(PACK):
-            z = sb("z%d" % u, [P, P * PACK], BF16)
+        z_tiles = [sb("z%d" % u, [P, P * PACK], BF16) for u in range(PACK)]
+
+        def gate(u):
             nc.vector.tensor_tensor(
-                z[:].rearrange("p (g i t) -> p g t i", i=4, t=PACK),
+                z_tiles[u][:].rearrange("p (g i t) -> p g t i", i=4, t=PACK),
                 sig[:].rearrange("p t (g u i) -> p u g t i", u=PACK, i=4)[:, u],
                 ga[:].rearrange("p t (g u i) -> p u g t i", u=PACK, i=4)[:, u],
                 ALU.mult,
             )
-            z_tiles.append(z)
-        for u in range(PACK):
+
+        def moments(u):
             z_codes = sb("z_codes%d" % u, [P, P], U32)
             z_scales = sb("z_scales%d" % u, [P, P], U8)
             quantise(z_codes[:], z_scales[:], z_tiles[u][:])
             product(banks_a[u][:], z_codes[:], z_scales[:], z2_codes[:], z2_scales[:])
 
+        for step in range(PACK + 1):
+            if step < PACK:
+                gate(step)
+            if step >= 1:
+                moments(step - 1)
+
         rows = out.rearrange("(g u i) n -> u g i n", u=PACK, i=4)
-        fetched = [sb("fetched%d" % u, [P, W], F32) for u in range(PACK)]
         result = [sb("result%d" % u, [P, W], F32) for u in range(PACK)]
 
         def fetch(u):
@@ -184,8 +205,14 @@ def tile_picked_momhopdhopb_none_p_kernel(
             nc.vector.tensor_tensor(second[u][:, :W], fetched[u][:], first[u][:, :W], ALU.max)
 
         def finish(u):
-            nc.vector.tensor_tensor(result[u][:], second[u][:].indirect(lists["n4"][:]), first[u][:, W:], ALU.subtract)
-            nc.sync.dma_start(rows[u], result[u][:])
+            pieces = 2 if u == PACK - 1 else 1
+            width = W // pieces
+            for j in range(pieces):
+                cols = slice(j * width, (j + 1) * width)
+                entries = lists["n4"][:, j * width // 16 : (j + 1) * width // 16]
+                half_cv = first[u][:, W + j * width : W + (j + 1) * width]
+                nc.vector.tensor_tensor(result[u][:, cols], second[u][:].indirect(entries), half_cv, ALU.subtract)
+                nc.sync.dma_start(rows[u][:, :, cols], result[u][:, cols])
 
         for step in range(PACK + 2):
             if step < PACK:

@@ -40,7 +40,7 @@ def tile_picked_momhopdhopb_none_p_kernel(
         xs = sb("xs", [P, T], U8)
         xw = sb("xw", [P, T], I32)
         wa_raw = [sb("wa_raw%d" % h, [P, PACK, HALF], F32) for h in range(2)]
-        wb_raw = [sb("wb_raw%d" % h, [P, PACK, HALF], F32) for h in range(2)]
+        wb_raw = sb("wb_raw", [P, PACK, N], F32)
         gains_in = sb("gains_in", [P, P], F32)
         gains = sb("gains", [P, 2 * PACK], F32)
         ident = sb("ident", [P, P], F32)
@@ -72,8 +72,7 @@ def tile_picked_momhopdhopb_none_p_kernel(
                 gains_in[PACK * j : PACK * (j + 1), :].rearrange("t (h e) -> t h e", e=8),
                 gain.rearrange("(h t e) o -> t h (e o)", t=PACK, e=8),
             )
-        load_half(wb_raw[0], wb, 0)
-        load_half(wb_raw[1], wb, 1)
+        nc.sync.dma_start(wb_raw[:], wb.rearrange("(p j) c -> p j c", j=PACK))
         nc.sync.dma_start(lists["n1"][:], n1)
         nc.sync.dma_start(lists["n2"][:], n2)
         nc.sync.dma_start(lists["n3"][:], n3)
@@ -98,7 +97,7 @@ def tile_picked_momhopdhopb_none_p_kernel(
             return dealt
 
         def weave(copy, name, raw):
-            woven = sb(name, [P, HALF * PACK], BF16)
+            woven = sb(name, [P, raw.shape[2] * PACK], BF16)
             copy(
                 woven[:].rearrange("p (c i j) -> p c j i", i=4, j=PACK),
                 raw[:].rearrange("p j (c i) -> p c j i", i=4),
@@ -114,7 +113,7 @@ def tile_picked_momhopdhopb_none_p_kernel(
         xs_a = pick_scales("offs")
         xs_b = pick_scales("two")
         wa_codes = sb("wa_codes", [P, W], U32)
-        wa_scales = sb("wa_scales", [P, W], U8)
+        wa_scales = sb("wa_scales", [P, W], U8, "got_offs")
         wa_lo = weave(nc.scalar.copy, "wa_lo", wa_raw[0])
         wa_hi = weave(nc.scalar.copy, "wa_hi", wa_raw[1])
         quantise(wa_codes[:, :HALF], wa_scales[:, :HALF], wa_lo[:])
@@ -150,10 +149,8 @@ def tile_picked_momhopdhopb_none_p_kernel(
 
         wb_codes = sb("wb_codes", [P, W], U32)
         wb_scales = sb("wb_scales", [P, W], U8)
-        wb_lo = weave(nc.vector.tensor_copy, "wb_lo", wb_raw[0])
-        wb_hi = weave(nc.vector.tensor_copy, "wb_hi", wb_raw[1])
-        quantise(wb_codes[:, :HALF], wb_scales[:, :HALF], wb_lo[:])
-        quantise(wb_codes[:, HALF:], wb_scales[:, HALF:], wb_hi[:])
+        wb_woven = weave(nc.vector.tensor_copy, "wb_woven", wb_raw)
+        quantise(wb_codes[:], wb_scales[:], wb_woven[:])
 
         z2 = sb("z2", [P, N, PACK], BF16, "last_a")
         for c in range(PACK):

from contextlib import ExitStack

import concourse.mybir as mybir
from concourse.masks import make_identity

K, T, S, N, H = 512, 2048, 512, 512, 512
FLOPS = 2 * K * S * H + 2 * K * S * N + 2 * S * H * N

F32 = mybir.dt.float32
BF16 = mybir.dt.bfloat16
I32 = mybir.dt.int32
U32 = mybir.dt.uint32
U16 = mybir.dt.uint16
U8 = mybir.dt.uint8
FP8X4 = mybir.dt.float8_e4m3fn_x4
ALU = mybir.AluOpType
ACT = mybir.ActivationFunctionType

P = 128
PACK = 4
W = 512
HALF = W // 2


def tile_picked_momhopdhopb_none_p_kernel(
    tc, x_words, x_scales, wa, wb, gt, gi, offs, two, n1, n2, n3, n4, out
):
    nc = tc.nc
    with ExitStack() as ctx:
        keep = ctx.enter_context(tc.tile_pool(name="keep", bufs=1))
        psum = ctx.enter_context(tc.psum_pool(name="psum", bufs=1))

        def sb(name, shape, dtype, tag=None):
            return keep.tile(shape, dtype, name=name, tag=tag or name, align_bytes=64)

        lists = {}
        for name in ("offs", "two", "n1", "n2", "n3", "n4"):
            lists[name] = sb("list_" + name, [P, W // 16], U16)

        xs = sb("xs", [P, T], U8)
        xw = sb("xw", [P, T], I32)
        wa_raw = [sb("wa_raw%d" % h, [P, PACK, HALF], F32) for h in range(2)]
        wb_raw = sb("wb_raw", [P, PACK, N], F32)
        gains_in = sb("gains_in", [P, P], F32)
        gains = sb("gains", [P, 2 * PACK], F32)
        ident = sb("ident", [P, P], F32)
        first = [sb("first%d" % t, [P, 2 * W], F32) for t in range(PACK)]
        second = [sb("second%d" % t, [P, 2 * W], F32) for t in range(PACK)]

        nc.vector.memset(xs[:].bitcast(I32), 0)
        warm = sb("warm", [P, 2], F32)
        nc.gpsimd.memset(warm[:, 0:1], 0.0)
        nc.scalar.activation(warm[:, 1:2], warm[:, 0:1], ACT.Sigmoid)
        for t in range(PACK):
            nc.vector.memset(first[t][:, W:], 0.0)
        nc.gpsimd.memset(gains_in[:], 0.0)
        make_identity(nc, ident[:])
        nc.gpsimd.memset(second[PACK - 1][:, W:], 0.0)

        def load_half(tile, w, h):
            nc.sync.dma_start(tile[:], w.rearrange("(p j) c -> p j c", j=PACK)[:, :, h * HALF : (h + 1) * HALF])

        load_half(wa_raw[0], wa, 0)
        for q in range(4):
            nc.sync.dma_start(xs[32 * q : 32 * q + 4, :].bitcast(I32), x_scales[0, 4 * q : 4 * q + 4, :].bitcast(I32))
        nc.sync.dma_start(lists["offs"][:], offs)
        load_half(wa_raw[1], wa, 1)
        nc.sync.dma_start(xw[:], x_words[0].rearrange("p n r -> p (n r)").bitcast(I32))
        nc.sync.dma_start(lists["two"][:], two)
        for j, gain in enumerate((gt, gi)):
            nc.sync.dma_start(
                gains_in[PACK * j : PACK * (j + 1), :].rearrange("t (h e) -> t h e", e=8),
                gain.rearrange("(h t e) o -> t h (e o)", t=PACK, e=8),
            )
        nc.sync.dma_start(wb_raw[:], wb.rearrange("(p j) c -> p j c", j=PACK))
        nc.sync.dma_start(lists["n1"][:], n1)
        nc.sync.dma_start(lists["n2"][:], n2)
        nc.sync.dma_start(lists["n3"][:], n3)
        nc.sync.dma_start(lists["n4"][:], n4)

        def pick_scales(name, tag=None):
            got = sb("got_" + name, [P, S], U8, tag)
            nc.vector.tensor_copy(got[:], xs[:].indirect(lists[name][:]))
            dealt = sb("xs_" + name, [P, S], U8)
            nc.vector.tensor_copy(
                dealt[:].bitcast(I32).rearrange("p (t h e) -> p t h e", t=PACK, e=2),
                got[:].bitcast(I32).rearrange("p (h t e) -> p t h e", t=PACK, e=2),
            )
            return dealt

        def pick_words(name, tag=None):
            dealt = sb("xw_" + name, [P, S], U32, tag)
            nc.vector.tensor_copy(
                dealt[:].rearrange("p (t h e) -> p h t e", t=PACK, e=8),
                xw[:].bitcast(U32).indirect(lists[name][:]),
            )
            return dealt

        def weave(copy, name, raw):
            woven = sb(name, [P, raw.shape[2] * PACK], BF16)
            copy(
                woven[:].rearrange("p (c i j) -> p c j i", i=4, j=PACK),
                raw[:].rearrange("p j (c i) -> p c j i", i=4),
            )
            return woven

        def quantise(codes, scales, woven):
            nc.vector.quantize_mx(out=codes.bitcast(FP8X4), scales=scales, in_=woven)

        def product(bank, lw, ls, rw, rs):
            nc.tensor.matmul_mx(out=bank, lhsT=lw.bitcast(FP8X4), lhsT_scale=ls, rhs=rw.bitcast(FP8X4), rhs_scale=rs, start=True, stop=True)

        xs_a = pick_scales("offs")
        xs_b = pick_scales("two")
        wa_codes = sb("wa_codes", [P, W], U32)
        wa_scales = sb("wa_scales", [P, W], U8, "got_offs")
        wa_lo = weave(nc.scalar.copy, "wa_lo", wa_raw[0])
        wa_hi = weave(nc.scalar.copy, "wa_hi", wa_raw[1])
        quantise(wa_codes[:, :HALF], wa_scales[:, :HALF], wa_lo[:])
        quantise(wa_codes[:, HALF:], wa_scales[:, HALF:], wa_hi[:])
        xw_a = pick_words("offs")
        xw_b = pick_words("two")

        banks_a = [psum.tile([P, W], F32, name="bank_a%d" % t) for t in range(PACK)]
        banks_b = [psum.tile([P, PACK, P], F32, name="bank_b%d" % c) for c in range(PACK)]
        for t in (1, 2, 3, 0):
            cols = slice(t * P, (t + 1) * P)
            product(banks_a[t][:], xw_a[:, cols], xs_a[:, cols], wa_codes[:], wa_scales[:])
        nc.tensor.transpose(banks_b[3][:, 0, :], gains_in[:], ident[:])

        sig = sb("sig", [P, PACK, W], F32)
        ga = sb("ga", [P, PACK, W], F32)
        fetched = [sb("fetched%d" % u, [P, W], F32) for u in range(PACK)]
        last_a = sb("last_a", [P, W], F32)
        again = [second[t][:, W:] for t in range(PACK - 1)] + [last_a[:]]
        for t in (1, 2, 3, 0):
            nc.scalar.copy(first[t][:, :W], banks_a[t][:])
            if t > 0:
                nc.sync.dma_start(again[t], first[t][:, :W])
            else:
                nc.scalar.copy(again[t], banks_a[t][:])
        for t in range(PACK):
            nc.vector.tensor_tensor(second[t][:, :W], first[t][:].indirect(lists["n1"][:]), again[t], ALU.subtract)
        nc.scalar.copy(gains[:], banks_b[3][:, 0, : 2 * PACK])
        for t in range(PACK):
            nc.scalar.activation(ga[:, t, :], banks_a[t][:], ACT.Copy, scale=gains[:, t : t + 1])
        for t in range(PACK):
            nc.scalar.activation(sig[:, t, :], second[t][:].indirect(lists["n2"][:]), ACT.Sigmoid)

        wb_codes = sb("wb_codes", [P, W], U32)
        wb_scales = sb("wb_scales", [P, W], U8)
        wb_woven = weave(nc.vector.tensor_copy, "wb_woven", wb_raw)
        quantise(wb_codes[:], wb_scales[:], wb_woven[:])

        z2 = sb("z2", [P, N, PACK], BF16, "last_a")
        for c in range(PACK):
            ccols = slice(c * P, (c + 1) * P)
            for t in range(PACK):
                cols = slice(t * P, (t + 1) * P)
                product(banks_b[c][:, t, :], xw_b[:, cols], xs_b[:, cols], wb_codes[:, ccols], wb_scales[:, ccols])
            nc.vector.tensor_tensor(
                z2[:, ccols, :],
                banks_b[c][:].rearrange("p t n -> p n t"),
                gains[:, PACK:].unsqueeze(1).to_broadcast([P, P, PACK]),
                ALU.mult,
            )
        z2_codes = sb("z2_codes", [P, N], U32)
        z2_scales = sb("z2_scales", [P, N], U8)
        quantise(z2_codes[:], z2_scales[:], z2[:].rearrange("p n t -> p (n t)"))

        z_tiles = [sb("z%d" % u, [P, P * PACK], BF16) for u in range(PACK)]

        def gate(u):
            nc.vector.tensor_tensor(
                z_tiles[u][:].rearrange("p (g i t) -> p g t i", i=4, t=PACK),
                sig[:].rearrange("p t (g u i) -> p u g t i", u=PACK, i=4)[:, u],
                ga[:].rearrange("p t (g u i) -> p u g t i", u=PACK, i=4)[:, u],
                ALU.mult,
            )

        def moments(u):
            z_codes = sb("z_codes%d" % u, [P, P], U32)
            z_scales = sb("z_scales%d" % u, [P, P], U8)
            quantise(z_codes[:], z_scales[:], z_tiles[u][:])
            product(banks_a[u][:], z_codes[:], z_scales[:], z2_codes[:], z2_scales[:])

        for step in range(PACK + 1):
            if step < PACK:
                gate(step)
            if step >= 1:
                moments(step - 1)

        rows = out.rearrange("(g u i) n -> u g i n", u=PACK, i=4)
        result = [sb("result%d" % u, [P, W], F32) for u in range(PACK)]

        def fetch(u):
            nc.scalar.activation(first[u][:, :W], banks_a[u][:], ACT.Copy, scale=0.0625)
            nc.vector.tensor_copy(fetched[u][:], first[u][:].indirect(lists["n3"][:]))
            nc.scalar.activation(first[u][:, W:], banks_a[u][:], ACT.Copy, scale=0.03125)

        def larger(u):
            nc.vector.tensor_tensor(second[u][:, :W], fetched[u][:], first[u][:, :W], ALU.max)

        def finish(u):
            pieces = 2 if u == PACK - 1 else 1
            width = W // pieces
            for j in range(pieces):
                cols = slice(j * width, (j + 1) * width)
                entries = lists["n4"][:, j * width // 16 : (j + 1) * width // 16]
                half_cv = first[u][:, W + j * width : W + (j + 1) * width]
                nc.vector.tensor_tensor(result[u][:, cols], second[u][:].indirect(entries), half_cv, ALU.subtract)
                nc.sync.dma_start(rows[u][:, :, cols], result[u][:, cols])

        for step in range(PACK + 2):
            if step < PACK:
                fetch(step)
            if 1 <= step <= PACK:
                larger(step - 1)
            if step >= 2:
                finish(step - 2)
